import numpy as np
import ml_dtypes


def mxq(x, axis, fmt="e4m3"):
    dtype, down = {"e4m3": (ml_dtypes.float8_e4m3fn, 7), "e5m2": (ml_dtypes.float8_e5m2, 14)}[fmt]
    v = np.moveaxis(np.asarray(x, np.float32).astype(ml_dtypes.bfloat16).astype(np.float64), axis, -1)
    blocks = v.reshape(v.shape[:-1] + (-1, 32))
    amax = np.abs(blocks).max(-1, keepdims=True)
    byte = np.maximum(np.where(amax > 0, np.frexp(amax)[1] - 1 + 127, 0) - down, 1)
    scale = np.exp2(byte - 127.0)
    codes = (blocks / scale).astype(np.float32).astype(dtype).astype(np.float64)
    return np.moveaxis((codes * scale).reshape(v.shape), -1, axis)


WIDE = False


def mx_kscale(k):
    if not WIDE:
        return np.ones(k)
    levels = np.array([10, -10, 5, -5, 0])
    if k % 512:
        return np.exp2(np.random.permutation(np.resize(levels, k // 32))).repeat(32)
    a = np.empty((k // 512, 16))
    for p in range(k // 512):
        a[p, :8] = np.random.permutation(np.resize(levels, 8))
        for g in range(8):
            far = levels[np.abs(levels - a[p, g]) >= 10]
            a[p, g + 8] = far[np.random.randint(len(far))]
    return np.exp2(a.ravel()).repeat(32)


def f64(x):
    return np.asarray(x).astype(np.float64)


def striped(idx):
    return np.tile(idx.reshape(-1, 16).T, (8, 1)).astype(np.uint16)


def unstriped(offs):
    return offs[:16].T.reshape(-1).astype(np.int64)


def striped8(idx):
    return np.concatenate([x.reshape(-1, 16).T for x in idx]).astype(np.uint16)


def runs(offs, k):
    lists = np.stack([offs[16 * r : 16 * r + 16].T.reshape(-1) for r in range(8)]).astype(np.int64)
    return lists[np.arange(k) % 512 // 64]


def pack_weight(w):
    k, n = w.shape
    w = f64(np.asarray(w, np.float32).astype(ml_dtypes.bfloat16)).reshape(k // 32, 32, n)
    amax = np.abs(w).max(1)
    byte = np.clip(np.where(amax > 0, np.frexp(amax)[1] - 1 + 127 - 7, 1), 1, 254)
    scaled = (w * np.exp2(127.0 - byte)[:, None, :]).reshape(k, n).astype(np.float32)
    words = np.ascontiguousarray(scaled.reshape(k // 512, 128, 4, n).transpose(0, 1, 3, 2)).astype(ml_dtypes.float8_e4m3fn).view(np.uint8)
    return words, np.ascontiguousarray(byte.astype(np.uint8).reshape(k // 512, 16, n))


def unpack_weight(words, scales):
    g, p, n, _ = words.shape
    vals = np.ascontiguousarray(words).view(ml_dtypes.float8_e4m3fn).astype(np.float64) * np.repeat(np.exp2(scales.astype(np.float64) - 127.0), 8, axis=1)[..., None]
    return vals.transpose(0, 1, 3, 2).reshape(g * 512, n)


def sigmoid(v):
    return 1.0 / (1.0 + np.exp(-np.maximum(v, -700.0)))

def planes(y):
    n, m = y.shape
    v = y.astype(np.float32).astype(ml_dtypes.bfloat16).astype(np.float64).reshape(n // 32, 32, m)
    top = np.abs(v).max(1)
    byte = np.clip(np.where(top > 0, np.frexp(top)[1] - 1 + 127 - 7, 1), 1, 254)
    codes = (v * np.exp2(127.0 - byte)[:, None, :]).reshape(n, m).astype(np.float32).astype(ml_dtypes.float8_e4m3fn).view(np.uint8)
    words = codes.reshape(n // 512, 128, 4, m).transpose(0, 1, 3, 2)
    return np.ascontiguousarray(words), np.ascontiguousarray(byte.astype(np.uint8).reshape(n // 512, 16, m))


K, T, S, N, H, W = 512, 2048, 512, 512, 512, 256


def setup_inputs():
    n = np.random.standard_normal
    s = mx_kscale(K)[:, None]
    u = mx_kscale(H)
    packed_xT = pack_weight(n((K, T)) * s)
    packed_w1 = pack_weight(n((K, H)) / np.sqrt(K) / s)
    packed_w2 = pack_weight(n((H, N)) / np.sqrt(2 * H) / u[:, None])
    packed_w3 = pack_weight(n((K, N)) / np.sqrt(2 * K) / s)
    perm = np.random.permutation(S)
    return {
        "x_words": packed_xT[0],
        "x_scales": packed_xT[1],
        "w1_words": packed_w1[0],
        "w1_scales": packed_w1[1],
        "gn": (np.random.uniform(0.5, 1.5, (H, 1)) * u[:, None]).astype(np.float32),
        "w2_words": packed_w2[0],
        "w2_scales": packed_w2[1],
        "w3_words": packed_w3[0],
        "w3_scales": packed_w3[1],
        "tau": np.random.uniform(0.3, 0.9, (N, 1)).astype(np.float32),
        "tau2": np.random.uniform(0.3, 0.9, (N, 1)).astype(np.float32),
        "offs": striped8(np.random.randint(0, T, (8, S))),
        "n1": striped(perm[:W]),
        "n2": striped(perm[W:]),
        "two": striped(np.random.permutation(T)[:S]),
        "n3": striped8(np.stack([np.random.permutation(S) for _ in range(8)])),
        "n4": striped8(np.stack([np.random.permutation(S) for _ in range(8)])),
    }


def reference(x_words, x_scales, w1_words, w1_scales, gn, w2_words, w2_scales, w3_words, w3_scales, tau, tau2, offs, n1, n2, two, n3, n4):
    xq = unpack_weight(x_words, x_scales)[np.arange(K)[:, None], runs(offs, K)]
    y = unpack_weight(w1_words, w1_scales).T @ xq
    pa = y[:, unstriped(n1)]
    pb = y[:, unstriped(n2)]
    ra = pa * sigmoid(pb)
    ds = y.copy()
    ds[:, unstriped(n2)] = ra
    z = f64(gn) * ds
    x_two = unpack_weight(x_words, x_scales)[:, unstriped(two)]
    h = unpack_weight(w2_words, w2_scales).T @ mxq(z, 0, "e4m3") + unpack_weight(w3_words, w3_scales).T @ x_two
    top = h.max(axis=1, keepdims=True)
    ea = np.exp(f64(tau) * (h[np.arange(N)[:, None], runs(n3, N)] - top))
    low = h.min(axis=1, keepdims=True)
    ea2 = np.exp(f64(tau2) * (low - (h[np.arange(N)[:, None], runs(n4, N)])))
    out_0 = 1.5 * (h * (ea + ea2))
    return (out_0,) + planes(out_0)

@@ -1,0 +1,263 @@
+from contextlib import ExitStack
+
+import concourse.mybir as mybir
+
+F32 = mybir.dt.float32
+BF16 = mybir.dt.bfloat16
+I32 = mybir.dt.int32
+U32 = mybir.dt.uint32
+U16 = mybir.dt.uint16
+U8 = mybir.dt.uint8
+FP8X4 = mybir.dt.float8_e4m3fn_x4
+ALU = mybir.AluOpType
+ACT = mybir.ActivationFunctionType
+AXIS = mybir.AxisListType
+
+P = 128
+T = 2048
+S = 512
+W = 256
+PACK = 4
+HALF = S // 2
+FLOPS = 3 * 2 * 512 * 512 * 512
+
+
+def words_view(dram):
+    return dram[0].rearrange("p n t -> p (n t)").bitcast(I32)
+
+
+def tile_picked_hmixfoldedf_none_po_kernel(
+    tc, x_words, x_scales, w1_words, w1_scales, gn, w2_words, w2_scales, w3_words, w3_scales,
+    tau, tau2, offs, n1, n2, two, n3, n4, out_0, out_1, out_2,
+):
+    nc = tc.nc
+    with ExitStack() as ctx:
+        keep = ctx.enter_context(tc.tile_pool(name="keep", bufs=1))
+        psum = ctx.enter_context(tc.psum_pool(name="psum", bufs=1))
+
+        def sb(name, shape, dtype):
+            return keep.tile(shape, dtype, name=name, align_bytes=64)
+
+        def load_list(name, dram):
+            tile = keep.tile(list(dram.shape), U16, name=name)
+            nc.sync.dma_start(tile[:], dram)
+            return tile
+
+        def load_words(name, dram):
+            tile = sb(name, [P, dram.shape[2]], U32)
+            nc.sync.dma_start(tile[:].bitcast(I32), words_view(dram))
+            return tile
+
+        def load_column(name, dram):
+            tile = sb(name, [P, PACK], F32)
+            nc.gpsimd.dma_start(tile[:], dram.rearrange("(p t) o -> p (t o)", t=PACK))
+            return tile
+
+        offs_t = load_list("offs_t", offs)
+        xs = sb("xs", [P, T], U8)
+        nc.sync.dma_start(
+            xs[:].bitcast(I32),
+            x_scales[0].bitcast(I32).unsqueeze(1).to_broadcast([16, 8, T // 4]),
+        )
+        two_t = load_list("two_t", two)
+        wraw = sb("wraw", [P, S], U8)
+        for q in range(4):
+            nc.sync.dma_start(
+                wraw[32 * q : 32 * q + 32, :].bitcast(I32),
+                w1_scales[0][4 * q : 4 * q + 4, :].bitcast(I32).unsqueeze(0).to_broadcast([8, 4, S // 4]),
+            )
+        xw = load_words("xw", x_words)
+        w1raw = load_words("w1raw", w1_words)
+
+        xq_plane = sb("xq_plane", [P, S], U8)
+        x2_plane = sb("x2_plane", [P, S], U8)
+        nc.gpsimd.memset(xq_plane[:].bitcast(I32), 0)
+        nc.gpsimd.memset(x2_plane[:].bitcast(I32), 0)
+        wraw23 = sb("wraw23", [P, S], U8)
+        nc.gpsimd.memset(wraw23[:].bitcast(I32), 0)
+        for k, dram in ((0, w2_scales), (4, w3_scales)):
+            for q in range(4):
+                nc.gpsimd.dma_start(
+                    wraw23[32 * q + k : 32 * q + k + 4, :].bitcast(I32), dram[0][4 * q : 4 * q + 4, :].bitcast(I32)
+                )
+        gn_t = load_column("gn_t", gn)
+        tau_t = load_column("tau_t", tau)
+        tau2_t = load_column("tau2_t", tau2)
+
+        def gather_scales(name, lst, plane, queue):
+            got = sb(name, [P, S], U8)
+            nc.vector.tensor_copy(got[:], xs[:].indirect(lst[:]))
+            for r in range(4):
+                queue.dma_start(plane[r:P:32, :].bitcast(I32), got[8 * r : P : 32, :].bitcast(I32))
+
+        def deal_scales(name, raw):
+            plane = sb(name, [P, S], U8)
+            nc.vector.tensor_copy(
+                plane[:].rearrange("p (t m) -> p t m", t=PACK), raw[:].rearrange("p (m t) -> p t m", t=PACK)
+            )
+            return plane
+
+        gather_scales("xq_got", offs_t, xq_plane, nc.scalar)
+        w1_plane = deal_scales("w1_plane", wraw)
+        xq = sb("xq", [P, S], U32)
+        nc.vector.tensor_copy(xq[:], xw[:].indirect(offs_t[:]))
+
+        n2_t = load_list("n2_t", n2)
+        n1_t = load_list("n1_t", n1)
+        w3raw = load_words("w3raw", w3_words)
+        w2raw = load_words("w2raw", w2_words)
+
+        w1 = sb("w1", [P, S], U32)
+        for t in range(PACK):
+            nc.scalar.copy(w1[:, t * P : (t + 1) * P], w1raw[:, t:S:PACK])
+
+        def deal_words(name, raw):
+            dealt = sb(name, [P, S], U32)
+            nc.scalar.copy(
+                dealt[:].rearrange("p (t c i) -> p c t i", t=PACK, i=4),
+                raw[:].rearrange("p (c i t) -> p c t i", t=PACK, i=4),
+            )
+            return dealt
+
+        y_ps = [psum.tile([P, S], F32, name="y_ps%d" % t) for t in range(PACK)]
+        h_ps = [psum.tile([P, S], F32, name="h_ps%d" % t) for t in range(PACK)]
+        for t in range(PACK):
+            cols = slice(t * P, (t + 1) * P)
+            nc.tensor.matmul_mx(
+                out=y_ps[t][:], lhsT=w1[:, cols].bitcast(FP8X4), lhsT_scale=w1_plane[:, cols],
+                rhs=xq[:].bitcast(FP8X4), rhs_scale=xq_plane[:], start=True, stop=True,
+            )
+
+        gather_scales("x2_got", two_t, x2_plane, nc.sync)
+        x2 = sb("x2", [P, S], U32)
+        nc.vector.tensor_copy(x2[:], xw[:].indirect(two_t[:]))
+        w3 = deal_words("w3", w3raw)
+        w2 = deal_words("w2", w2raw)
+        n3_t = load_list("n3_t", n3)
+        n4_t = load_list("n4_t", n4)
+
+        ds = [sb("ds%d" % t, [P, S], F32) for t in range(PACK)]
+        pa = [sb("pa%d" % t, [P, W], F32) for t in range(PACK)]
+        sg = [sb("sg%d" % t, [P, W], F32) for t in range(PACK)]
+        ra = sb("ra", [P, W], F32)
+        z_rows = sb("z_rows", [P, PACK, S], BF16)
+        z_in = sb("z_in", [P, S, PACK], BF16)
+        z_codes = sb("z_codes", [P, S], U32)
+        z_plane = sb("z_plane", [P, S], U8)
+
+        def fetch_pair(t):
+            nc.scalar.activation(sg[t][:], ds[t][:].indirect(n2_t[:]), ACT.Sigmoid)
+            nc.scalar.activation(pa[t][:], ds[t][:].indirect(n1_t[:]), ACT.Copy)
+
+        def scatter_product(t):
+            nc.vector.tensor_tensor(ds[t][:].indirect(n2_t[:]), pa[t][:], sg[t][:], ALU.mult)
+
+        for t in range(PACK - 1):
+            nc.vector.tensor_copy(ds[t][:], y_ps[t][:])
+        fetch_pair(0)
+        fetch_pair(1)
+        nc.scalar.copy(ds[3][:], y_ps[3][:])
+        fetch_pair(3)
+        fetch_pair(2)
+        scatter_product(0)
+        w23_plane = deal_scales("w23_plane", wraw23)
+        for t in range(PACK):
+            cols = slice(t * P, (t + 1) * P)
+            nc.tensor.matmul_mx(
+                out=h_ps[t][:], lhsT=w3[:, cols].bitcast(FP8X4), lhsT_scale=w23_plane[4:P, cols],
+                rhs=x2[:].bitcast(FP8X4), rhs_scale=x2_plane[:], start=True, stop=False,
+            )
+        scatter_product(1)
+        nc.vector.tensor_tensor(ra[:], pa[3][:], sg[3][:], ALU.mult)
+        nc.scalar.activation(ds[3][:].indirect(n2_t[:]), ra[:], ACT.Copy)
+        scatter_product(2)
+        for t in range(PACK - 1):
+            nc.vector.tensor_scalar(z_rows[:, t, :], ds[t][:], gn_t[:, t : t + 1], None, ALU.mult)
+        nc.scalar.activation(z_rows[:, 3, :], ds[3][:], ACT.Copy, scale=gn_t[:, 3:4])
+
+        def weave(copy, dst, src, lo, hi):
+            copy(
+                dst[:, lo:hi, :].rearrange("p (c i) t -> p c t i", i=4),
+                src[:, :, lo:hi].rearrange("p t (c i) -> p c t i", i=4),
+            )
+
+        def quantise(codes, plane, src, lo, hi):
+            nc.vector.quantize_mx(
+                out=codes[:, lo:hi].bitcast(FP8X4), scales=plane[:, lo:hi],
+                in_=src[:, lo:hi, :].rearrange("p j t -> p (j t)"),
+            )
+
+        weave(nc.vector.tensor_copy, z_in, z_rows, 0, 256)
+        weave(nc.scalar.copy, z_in, z_rows, 384, 512)
+        weave(nc.vector.tensor_copy, z_in, z_rows, 256, 384)
+        quantise(z_codes, z_plane, z_in, 0, HALF)
+        quantise(z_codes, z_plane, z_in, HALF, S)
+        for t in range(PACK):
+            cols = slice(t * P, (t + 1) * P)
+            for half in range(2):
+                js = slice(half * HALF, (half + 1) * HALF)
+                nc.tensor.matmul_mx(
+                    out=h_ps[t][:, js], lhsT=w2[:, cols].bitcast(FP8X4), lhsT_scale=w23_plane[:, cols],
+                    rhs=z_codes[:, js].bitcast(FP8X4), rhs_scale=z_plane[:, js], start=False, stop=(half == 1),
+                )
+
+        neg_tau2 = sb("neg_tau2", [P, PACK], F32)
+        nc.vector.tensor_scalar(neg_tau2[:], tau2_t[:], -1.0, None, ALU.mult)
+        h = [sb("h%d" % t, [P, S], F32) for t in range(PACK)]
+        ea = [sb("ea%d" % t, [P, S], F32) for t in range(PACK)]
+        ea2 = [sb("ea2%d" % t, [P, S], F32) for t in range(PACK)]
+        both = [sb("both%d" % t, [P, S], F32) for t in range(PACK)]
+        top = [sb("top%d" % t, [P, 1], F32) for t in range(PACK)]
+        low = [sb("low%d" % t, [P, 1], F32) for t in range(PACK)]
+        top_bias = [sb("top_bias%d" % t, [P, 1], F32) for t in range(PACK)]
+        low_bias = [sb("low_bias%d" % t, [P, 1], F32) for t in range(PACK)]
+        res = sb("res", [P, PACK, S], F32)
+        o_in = sb("o_in", [P, S, PACK], BF16)
+        o_codes = sb("o_codes", [P, S], U32)
+        o_plane = sb("o_plane", [P, S], U8)
+        out_rows = out_0.rearrange("(p t) j -> p t j", t=PACK)
+
+        for t in range(PACK):
+            nc.vector.tensor_scalar(h[t][:], h_ps[t][:], 1.0, None, ALU.mult, ALU.max, accum_out=top[t][:])
+            nc.vector.tensor_scalar(top_bias[t][:], top[t][:], tau_t[:, t : t + 1], -1.0, ALU.mult, ALU.mult)
+            nc.vector.tensor_reduce(low[t][:], h_ps[t][:], AXIS.X, ALU.min)
+            nc.vector.tensor_scalar(low_bias[t][:], low[t][:], tau2_t[:, t : t + 1], None, ALU.mult)
+
+        def fetch_top(t, lo, hi):
+            nc.scalar.activation(
+                ea[t][:, lo:hi], h[t][:].indirect(n3_t[:, lo // 16 : hi // 16]), ACT.Exp,
+                bias=top_bias[t][:], scale=tau_t[:, t : t + 1],
+            )
+
+        def fetch_low(t, lo, hi):
+            nc.scalar.activation(
+                ea2[t][:, lo:hi], h[t][:].indirect(n4_t[:, lo // 16 : hi // 16]), ACT.Exp,
+                bias=low_bias[t][:], scale=neg_tau2[:, t : t + 1],
+            )
+
+        def combine(t, lo, hi):
+            nc.vector.tensor_tensor(both[t][:, lo:hi], ea[t][:, lo:hi], ea2[t][:, lo:hi], ALU.add)
+            nc.vector.scalar_tensor_tensor(
+                res[:, t, lo:hi], h[t][:, lo:hi], 1.5, both[t][:, lo:hi], ALU.mult, ALU.mult
+            )
+
+        for t in range(2):
+            for lo in (0, HALF):
+                fetch_top(t, lo, lo + HALF)
+            for lo in (0, HALF):
+                fetch_low(t, lo, lo + HALF)
+            combine(t, 0, S)
+            nc.sync.dma_start(out_rows[:, t, :], res[:, t, :])
+        codes_out = words_view(out_1)
+        for lo, hi in ((0, 256), (256, 384), (384, 512)):
+            for t in range(2, PACK):
+                fetch_top(t, lo, hi)
+                fetch_low(t, lo, hi)
+                combine(t, lo, hi)
+            nc.sync.dma_start(out_rows[:, 2:PACK, lo:hi], res[:, 2:PACK, lo:hi])
+            weave(nc.vector.tensor_copy, o_in, res, lo, hi)
+            quantise(o_codes, o_plane, o_in, lo, hi)
+            nc.sync.dma_start(codes_out[:, lo:hi], o_codes[:, lo:hi].bitcast(I32))
+        for r in range(4):
+            queue = nc.scalar if r % 2 else nc.sync
+            queue.dma_start(out_2[0][r:16:4, :].bitcast(I32), o_plane[r:P:32, :].bitcast(I32))

@@ -35,8 +35,8 @@ def tile_picked_hmixfoldedf_none_po_kernel(
         keep = ctx.enter_context(tc.tile_pool(name="keep", bufs=1))
         psum = ctx.enter_context(tc.psum_pool(name="psum", bufs=1))
 
-        def sb(name, shape, dtype):
-            return keep.tile(shape, dtype, name=name, align_bytes=64)
+        def sb(name, shape, dtype, tag=""):
+            return keep.tile(shape, dtype, name=name, tag=tag or name, align_bytes=64)
 
         def load_list(name, dram):
             tile = keep.tile(list(dram.shape), U16, name=name)
@@ -73,16 +73,16 @@ def tile_picked_hmixfoldedf_none_po_kernel(
         x2_plane = sb("x2_plane", [P, S], U8)
         nc.gpsimd.memset(xq_plane[:].bitcast(I32), 0)
         nc.gpsimd.memset(x2_plane[:].bitcast(I32), 0)
-        wraw23 = sb("wraw23", [P, S], U8)
-        nc.gpsimd.memset(wraw23[:].bitcast(I32), 0)
-        for k, dram in ((0, w2_scales), (4, w3_scales)):
-            for q in range(4):
-                nc.gpsimd.dma_start(
-                    wraw23[32 * q + k : 32 * q + k + 4, :].bitcast(I32), dram[0][4 * q : 4 * q + 4, :].bitcast(I32)
-                )
+        h = [sb("h%d" % t, [P, 2 * S if t < 2 else S], F32) for t in range(PACK)]
+        for t in range(2):
+            nc.gpsimd.memset(h[t][:, S:], 0.0)
         gn_t = load_column("gn_t", gn)
         tau_t = load_column("tau_t", tau)
         tau2_t = load_column("tau2_t", tau2)
+        neg_tau = sb("neg_tau", [P, PACK], F32)
+        nc.gpsimd.tensor_scalar(neg_tau[:], tau_t[:], -1.0, 0.0, ALU.mult, ALU.add)
+        neg_tau2 = sb("neg_tau2", [P, PACK], F32)
+        nc.gpsimd.tensor_scalar(neg_tau2[:], tau2_t[:], -1.0, 0.0, ALU.mult, ALU.add)
 
         def gather_scales(name, lst, plane, queue):
             got = sb(name, [P, S], U8)
@@ -90,15 +90,15 @@ def tile_picked_hmixfoldedf_none_po_kernel(
             for r in range(4):
                 queue.dma_start(plane[r:P:32, :].bitcast(I32), got[8 * r : P : 32, :].bitcast(I32))
 
-        def deal_scales(name, raw):
+        def deal_scales(name, raw, engine):
             plane = sb(name, [P, S], U8)
-            nc.vector.tensor_copy(
+            engine.tensor_copy(
                 plane[:].rearrange("p (t m) -> p t m", t=PACK), raw[:].rearrange("p (m t) -> p t m", t=PACK)
             )
             return plane
 
         gather_scales("xq_got", offs_t, xq_plane, nc.scalar)
-        w1_plane = deal_scales("w1_plane", wraw)
+        w1_plane = deal_scales("w1_plane", wraw, nc.vector)
         xq = sb("xq", [P, S], U32)
         nc.vector.tensor_copy(xq[:], xw[:].indirect(offs_t[:]))
 
@@ -133,6 +133,11 @@ def tile_picked_hmixfoldedf_none_po_kernel(
         nc.vector.tensor_copy(x2[:], xw[:].indirect(two_t[:]))
         w3 = deal_words("w3", w3raw)
         w2 = deal_words("w2", w2raw)
+        for k, dram in ((4, w3_scales), (8, w2_scales)):
+            for q in range(4):
+                nc.sync.dma_start(
+                    wraw[32 * q + k : 32 * q + k + 4, :].bitcast(I32), dram[0][4 * q : 4 * q + 4, :].bitcast(I32)
+                )
         n3_t = load_list("n3_t", n3)
         n4_t = load_list("n4_t", n4)
 
@@ -141,7 +146,6 @@ def tile_picked_hmixfoldedf_none_po_kernel(
         sg = [sb("sg%d" % t, [P, W], F32) for t in range(PACK)]
         ra = sb("ra", [P, W], F32)
         z_rows = sb("z_rows", [P, PACK, S], BF16)
-        z_in = sb("z_in", [P, S, PACK], BF16)
         z_codes = sb("z_codes", [P, S], U32)
         z_plane = sb("z_plane", [P, S], U8)
 
@@ -152,28 +156,34 @@ def tile_picked_hmixfoldedf_none_po_kernel(
         def scatter_product(t):
             nc.vector.tensor_tensor(ds[t][:].indirect(n2_t[:]), pa[t][:], sg[t][:], ALU.mult)
 
-        for t in range(PACK - 1):
-            nc.vector.tensor_copy(ds[t][:], y_ps[t][:])
+        def scale_rows_vector(t):
+            nc.vector.tensor_scalar(z_rows[:, t, :], ds[t][:], gn_t[:, t : t + 1], None, ALU.mult)
+
+        nc.scalar.copy(ds[0][:], y_ps[0][:])
+        nc.vector.tensor_copy(ds[1][:], y_ps[1][:])
+        nc.vector.tensor_copy(ds[2][:], y_ps[2][:])
         fetch_pair(0)
         fetch_pair(1)
         nc.scalar.copy(ds[3][:], y_ps[3][:])
-        fetch_pair(3)
         fetch_pair(2)
+        fetch_pair(3)
         scatter_product(0)
-        w23_plane = deal_scales("w23_plane", wraw23)
+        scatter_product(1)
+        nc.vector.tensor_tensor(ra[:], pa[2][:], sg[2][:], ALU.mult)
+        nc.scalar.activation(ds[2][:].indirect(n2_t[:]), ra[:], ACT.Copy)
+        scale_rows_vector(0)
+        scale_rows_vector(1)
+        scatter_product(3)
+        nc.scalar.activation(z_rows[:, 2, :], ds[2][:], ACT.Copy, scale=gn_t[:, 2:3])
+        scale_rows_vector(3)
+        w23_plane = deal_scales("w23_plane", wraw, nc.gpsimd)
         for t in range(PACK):
             cols = slice(t * P, (t + 1) * P)
             nc.tensor.matmul_mx(
                 out=h_ps[t][:], lhsT=w3[:, cols].bitcast(FP8X4), lhsT_scale=w23_plane[4:P, cols],
                 rhs=x2[:].bitcast(FP8X4), rhs_scale=x2_plane[:], start=True, stop=False,
             )
-        scatter_product(1)
-        nc.vector.tensor_tensor(ra[:], pa[3][:], sg[3][:], ALU.mult)
-        nc.scalar.activation(ds[3][:].indirect(n2_t[:]), ra[:], ACT.Copy)
-        scatter_product(2)
-        for t in range(PACK - 1):
-            nc.vector.tensor_scalar(z_rows[:, t, :], ds[t][:], gn_t[:, t : t + 1], None, ALU.mult)
-        nc.scalar.activation(z_rows[:, 3, :], ds[3][:], ACT.Copy, scale=gn_t[:, 3:4])
+        z_in = sb("z_in", [P, S, PACK], BF16)
 
         def weave(copy, dst, src, lo, hi):
             copy(
@@ -187,9 +197,8 @@ def tile_picked_hmixfoldedf_none_po_kernel(
                 in_=src[:, lo:hi, :].rearrange("p j t -> p (j t)"),
             )
 
-        weave(nc.vector.tensor_copy, z_in, z_rows, 0, 256)
-        weave(nc.scalar.copy, z_in, z_rows, 384, 512)
-        weave(nc.vector.tensor_copy, z_in, z_rows, 256, 384)
+        weave(nc.vector.tensor_copy, z_in, z_rows, 0, HALF)
+        weave(nc.scalar.copy, z_in, z_rows, HALF, S)
         quantise(z_codes, z_plane, z_in, 0, HALF)
         quantise(z_codes, z_plane, z_in, HALF, S)
         for t in range(PACK):
@@ -197,16 +206,12 @@ def tile_picked_hmixfoldedf_none_po_kernel(
             for half in range(2):
                 js = slice(half * HALF, (half + 1) * HALF)
                 nc.tensor.matmul_mx(
-                    out=h_ps[t][:, js], lhsT=w2[:, cols].bitcast(FP8X4), lhsT_scale=w23_plane[:, cols],
+                    out=h_ps[t][:, js], lhsT=w2[:, cols].bitcast(FP8X4), lhsT_scale=w23_plane[8:P, cols],
                     rhs=z_codes[:, js].bitcast(FP8X4), rhs_scale=z_plane[:, js], start=False, stop=(half == 1),
                 )
 
-        neg_tau2 = sb("neg_tau2", [P, PACK], F32)
-        nc.vector.tensor_scalar(neg_tau2[:], tau2_t[:], -1.0, None, ALU.mult)
-        h = [sb("h%d" % t, [P, S], F32) for t in range(PACK)]
         ea = [sb("ea%d" % t, [P, S], F32) for t in range(PACK)]
         ea2 = [sb("ea2%d" % t, [P, S], F32) for t in range(PACK)]
-        both = [sb("both%d" % t, [P, S], F32) for t in range(PACK)]
         top = [sb("top%d" % t, [P, 1], F32) for t in range(PACK)]
         low = [sb("low%d" % t, [P, 1], F32) for t in range(PACK)]
         top_bias = [sb("top_bias%d" % t, [P, 1], F32) for t in range(PACK)]
@@ -218,10 +223,11 @@ def tile_picked_hmixfoldedf_none_po_kernel(
         out_rows = out_0.rearrange("(p t) j -> p t j", t=PACK)
 
         for t in range(PACK):
-            nc.vector.tensor_scalar(h[t][:], h_ps[t][:], 1.0, None, ALU.mult, ALU.max, accum_out=top[t][:])
-            nc.vector.tensor_scalar(top_bias[t][:], top[t][:], tau_t[:, t : t + 1], -1.0, ALU.mult, ALU.mult)
+            nc.vector.tensor_scalar(h[t][:, :S], h_ps[t][:], 1.0, None, ALU.mult, ALU.max, accum_out=top[t][:])
+            nc.gpsimd.tensor_scalar(top_bias[t][:], top[t][:], neg_tau[:, t : t + 1], 0.0, ALU.mult, ALU.add)
             nc.vector.tensor_reduce(low[t][:], h_ps[t][:], AXIS.X, ALU.min)
-            nc.vector.tensor_scalar(low_bias[t][:], low[t][:], tau2_t[:, t : t + 1], None, ALU.mult)
+            nc.gpsimd.tensor_scalar(low_bias[t][:], low[t][:], tau2_t[:, t : t + 1], 0.0, ALU.mult, ALU.add)
+        both = [sb("both%d" % t, [P, S], F32, "low3" if t == 0 else "") for t in range(PACK)]
 
         def fetch_top(t, lo, hi):
             nc.scalar.activation(
@@ -242,10 +248,8 @@ def tile_picked_hmixfoldedf_none_po_kernel(
             )
 
         for t in range(2):
-            for lo in (0, HALF):
-                fetch_top(t, lo, lo + HALF)
-            for lo in (0, HALF):
-                fetch_low(t, lo, lo + HALF)
+            fetch_top(t, 0, S)
+            fetch_low(t, 0, S)
             combine(t, 0, S)
             nc.sync.dma_start(out_rows[:, t, :], res[:, t, :])
         codes_out = words_view(out_1)

@@ -53,6 +53,10 @@ def tile_picked_hmixfoldedf_none_po_kernel(
             nc.gpsimd.dma_start(tile[:], dram.rearrange("(p t) o -> p (t o)", t=PACK))
             return tile
 
+        warm_in = sb("warm_in", [P, 1], F32)
+        warm_out = sb("warm_out", [P, 1], F32)
+        nc.vector.memset(warm_in[:], 0.0)
+        nc.scalar.activation(warm_out[:], warm_in[:], ACT.Sigmoid)
         offs_t = load_list("offs_t", offs)
         xs = sb("xs", [P, T], U8)
         nc.sync.dma_start(

@@ -14,11 +14,21 @@ ACT = mybir.ActivationFunctionType
 AXIS = mybir.AxisListType
 
 P = 128
-T = 2048
-S = 512
-W = 256
+TOKENS = 2048
+COLS = 512
+PAIRS = 256
 PACK = 4
-HALF = S // 2
+INT_BYTES = 4
+QUADS = 4
+QUAD_BLOCKS = 4
+BLOCKS = 16
+LIST_ROWS = 16
+RUN = 4
+HALF = COLS // 2
+W3_PLANE = 4
+W2_PLANE = 8
+WHOLE_TILES = 2
+PIECES = ((0, 256), (256, 384), (384, 512))
 FLOPS = 3 * 2 * 512 * 512 * 512
 
 
@@ -57,74 +67,76 @@ def tile_picked_hmixfoldedf_none_po_kernel(
         warm_out = sb("warm_out", [P, 1], F32)
         nc.vector.memset(warm_in[:], 0.0)
         nc.scalar.activation(warm_out[:], warm_in[:], ACT.Sigmoid)
-        offs_t = load_list("offs_t", offs)
-        xs = sb("xs", [P, T], U8)
-        nc.sync.dma_start(
-            xs[:].bitcast(I32),
-            x_scales[0].bitcast(I32).unsqueeze(1).to_broadcast([16, 8, T // 4]),
-        )
-        two_t = load_list("two_t", two)
-        wraw = sb("wraw", [P, S], U8)
-        for q in range(4):
-            nc.sync.dma_start(
-                wraw[32 * q : 32 * q + 32, :].bitcast(I32),
-                w1_scales[0][4 * q : 4 * q + 4, :].bitcast(I32).unsqueeze(0).to_broadcast([8, 4, S // 4]),
-            )
-        xw = load_words("xw", x_words)
-        w1raw = load_words("w1raw", w1_words)
 
-        xq_plane = sb("xq_plane", [P, S], U8)
-        x2_plane = sb("x2_plane", [P, S], U8)
+        offs_list = load_list("offs_list", offs)
+        x_scale_rows = sb("x_scale_rows", [P, TOKENS], U8)
+        nc.sync.dma_start(
+            x_scale_rows[:].bitcast(I32),
+            x_scales[0].bitcast(I32).unsqueeze(1).to_broadcast([BLOCKS, P // BLOCKS, TOKENS // INT_BYTES]),
+        )
+        two_list = load_list("two_list", two)
+        w_scale_rows = sb("w_scale_rows", [P, COLS], U8)
+        for q in range(QUADS):
+            nc.sync.dma_start(
+                w_scale_rows[32 * q : 32 * q + 32, :].bitcast(I32),
+                w1_scales[0][4 * q : 4 * q + 4, :].bitcast(I32).unsqueeze(0).to_broadcast([8, QUAD_BLOCKS, COLS // INT_BYTES]),
+            )
+        x_table = load_words("x_table", x_words)
+        w1_raw = load_words("w1_raw", w1_words)
+
+        xq_plane = sb("xq_plane", [P, COLS], U8)
+        x2_plane = sb("x2_plane", [P, COLS], U8)
         nc.gpsimd.memset(xq_plane[:].bitcast(I32), 0)
         nc.gpsimd.memset(x2_plane[:].bitcast(I32), 0)
-        h = [sb("h%d" % t, [P, 2 * S if t < 2 else S], F32) for t in range(PACK)]
-        for t in range(2):
-            nc.gpsimd.memset(h[t][:, S:], 0.0)
-        gn_t = load_column("gn_t", gn)
-        tau_t = load_column("tau_t", tau)
-        tau2_t = load_column("tau2_t", tau2)
+        h = [sb("h%d" % t, [P, 2 * COLS if t < WHOLE_TILES else COLS], F32) for t in range(PACK)]
+        for t in range(WHOLE_TILES):
+            nc.gpsimd.memset(h[t][:, COLS:], 0.0)
+        gn_col = load_column("gn_col", gn)
+        tau_col = load_column("tau_col", tau)
+        tau2_col = load_column("tau2_col", tau2)
         neg_tau = sb("neg_tau", [P, PACK], F32)
-        nc.gpsimd.tensor_scalar(neg_tau[:], tau_t[:], -1.0, 0.0, ALU.mult, ALU.add)
+        nc.gpsimd.tensor_scalar(neg_tau[:], tau_col[:], -1.0, 0.0, ALU.mult, ALU.add)
         neg_tau2 = sb("neg_tau2", [P, PACK], F32)
-        nc.gpsimd.tensor_scalar(neg_tau2[:], tau2_t[:], -1.0, 0.0, ALU.mult, ALU.add)
+        nc.gpsimd.tensor_scalar(neg_tau2[:], tau2_col[:], -1.0, 0.0, ALU.mult, ALU.add)
 
-        def gather_scales(name, lst, plane, queue):
-            got = sb(name, [P, S], U8)
-            nc.vector.tensor_copy(got[:], xs[:].indirect(lst[:]))
-            for r in range(4):
-                queue.dma_start(plane[r:P:32, :].bitcast(I32), got[8 * r : P : 32, :].bitcast(I32))
+        def gather_scales(name, offsets, plane, queue):
+            picked = sb(name, [P, COLS], U8)
+            nc.vector.tensor_copy(picked[:], x_scale_rows[:].indirect(offsets[:]))
+            for r in range(QUAD_BLOCKS):
+                queue.dma_start(plane[r:P:32, :].bitcast(I32), picked[8 * r : P : 32, :].bitcast(I32))
 
-        def deal_scales(name, raw, engine):
-            plane = sb(name, [P, S], U8)
+        def deal_scales(name, engine):
+            plane = sb(name, [P, COLS], U8)
             engine.tensor_copy(
-                plane[:].rearrange("p (t m) -> p t m", t=PACK), raw[:].rearrange("p (m t) -> p t m", t=PACK)
+                plane[:].rearrange("p (t m) -> p t m", t=PACK),
+                w_scale_rows[:].rearrange("p (m t) -> p t m", t=PACK),
             )
             return plane
 
-        gather_scales("xq_got", offs_t, xq_plane, nc.scalar)
-        w1_plane = deal_scales("w1_plane", wraw, nc.vector)
-        xq = sb("xq", [P, S], U32)
-        nc.vector.tensor_copy(xq[:], xw[:].indirect(offs_t[:]))
-
-        n2_t = load_list("n2_t", n2)
-        n1_t = load_list("n1_t", n1)
-        w3raw = load_words("w3raw", w3_words)
-        w2raw = load_words("w2raw", w2_words)
-
-        w1 = sb("w1", [P, S], U32)
-        for t in range(PACK):
-            nc.scalar.copy(w1[:, t * P : (t + 1) * P], w1raw[:, t:S:PACK])
-
-        def deal_words(name, raw):
-            dealt = sb(name, [P, S], U32)
-            nc.scalar.copy(
-                dealt[:].rearrange("p (t c i) -> p c t i", t=PACK, i=4),
-                raw[:].rearrange("p (c i t) -> p c t i", t=PACK, i=4),
+        def deal_words(name, raw, copy, dtype):
+            dealt = sb(name, [P, COLS], U32)
+            copy(
+                dealt[:].bitcast(dtype).rearrange("p (t c i) -> p c t i", t=PACK, i=RUN),
+                raw[:].bitcast(dtype).rearrange("p (c i t) -> p c t i", t=PACK, i=RUN),
             )
             return dealt
 
-        y_ps = [psum.tile([P, S], F32, name="y_ps%d" % t) for t in range(PACK)]
-        h_ps = [psum.tile([P, S], F32, name="h_ps%d" % t) for t in range(PACK)]
+        gather_scales("xq_picked", offs_list, xq_plane, nc.scalar)
+        w1_plane = deal_scales("w1_plane", nc.vector)
+        xq = sb("xq", [P, COLS], U32)
+        nc.vector.tensor_copy(xq[:], x_table[:].indirect(offs_list[:]))
+
+        n2_list = load_list("n2_list", n2)
+        n1_list = load_list("n1_list", n1)
+        w3_raw = load_words("w3_raw", w3_words)
+        w2_raw = load_words("w2_raw", w2_words)
+
+        w1 = sb("w1", [P, COLS], U32)
+        for t in range(PACK):
+            nc.scalar.copy(w1[:, t * P : (t + 1) * P], w1_raw[:, t:COLS:PACK])
+
+        y_ps = [psum.tile([P, COLS], F32, name="y_ps%d" % t) for t in range(PACK)]
+        h_ps = [psum.tile([P, COLS], F32, name="h_ps%d" % t) for t in range(PACK)]
         for t in range(PACK):
             cols = slice(t * P, (t + 1) * P)
             nc.tensor.matmul_mx(
@@ -132,40 +144,41 @@ def tile_picked_hmixfoldedf_none_po_kernel(
                 rhs=xq[:].bitcast(FP8X4), rhs_scale=xq_plane[:], start=True, stop=True,
             )
 
-        gather_scales("x2_got", two_t, x2_plane, nc.sync)
-        x2 = sb("x2", [P, S], U32)
-        nc.vector.tensor_copy(x2[:], xw[:].indirect(two_t[:]))
-        w3 = deal_words("w3", w3raw)
-        w2 = deal_words("w2", w2raw)
-        for k, dram in ((4, w3_scales), (8, w2_scales)):
-            for q in range(4):
+        gather_scales("x2_picked", two_list, x2_plane, nc.sync)
+        x2 = sb("x2", [P, COLS], U32)
+        nc.vector.tensor_copy(x2[:], x_table[:].indirect(two_list[:]))
+        w3 = deal_words("w3", w3_raw, nc.scalar.copy, U32)
+        for k, dram in ((W3_PLANE, w3_scales), (W2_PLANE, w2_scales)):
+            for q in range(QUADS):
                 nc.sync.dma_start(
-                    wraw[32 * q + k : 32 * q + k + 4, :].bitcast(I32), dram[0][4 * q : 4 * q + 4, :].bitcast(I32)
+                    w_scale_rows[32 * q + k : 32 * q + k + 4, :].bitcast(I32),
+                    dram[0][4 * q : 4 * q + 4, :].bitcast(I32),
                 )
-        n3_t = load_list("n3_t", n3)
-        n4_t = load_list("n4_t", n4)
+        n3_list = load_list("n3_list", n3)
+        n4_list = load_list("n4_list", n4)
 
-        ds = [sb("ds%d" % t, [P, S], F32) for t in range(PACK)]
-        pa = [sb("pa%d" % t, [P, W], F32) for t in range(PACK)]
-        sg = [sb("sg%d" % t, [P, W], F32) for t in range(PACK)]
-        ra = sb("ra", [P, W], F32)
-        z_rows = sb("z_rows", [P, PACK, S], BF16)
-        z_codes = sb("z_codes", [P, S], U32)
-        z_plane = sb("z_plane", [P, S], U8)
+        ds = [sb("ds%d" % t, [P, COLS], F32) for t in range(PACK)]
+        pa = [sb("pa%d" % t, [P, PAIRS], F32) for t in range(PACK)]
+        gate = [sb("gate%d" % t, [P, PAIRS], F32) for t in range(PACK)]
+        ra = sb("ra", [P, PAIRS], F32)
+        z_rows = sb("z_rows", [P, PACK, COLS], BF16)
+        z_codes = sb("z_codes", [P, COLS], U32)
+        z_plane = sb("z_plane", [P, COLS], U8)
 
         def fetch_pair(t):
-            nc.scalar.activation(sg[t][:], ds[t][:].indirect(n2_t[:]), ACT.Sigmoid)
-            nc.scalar.activation(pa[t][:], ds[t][:].indirect(n1_t[:]), ACT.Copy)
+            nc.scalar.activation(gate[t][:], ds[t][:].indirect(n2_list[:]), ACT.Sigmoid)
+            nc.scalar.activation(pa[t][:], ds[t][:].indirect(n1_list[:]), ACT.Copy)
 
         def scatter_product(t):
-            nc.vector.tensor_tensor(ds[t][:].indirect(n2_t[:]), pa[t][:], sg[t][:], ALU.mult)
+            nc.vector.tensor_tensor(ds[t][:].indirect(n2_list[:]), pa[t][:], gate[t][:], ALU.mult)
 
-        def scale_rows_vector(t):
-            nc.vector.tensor_scalar(z_rows[:, t, :], ds[t][:], gn_t[:, t : t + 1], None, ALU.mult)
+        def gain_and_round(t):
+            nc.vector.tensor_scalar(z_rows[:, t, :], ds[t][:], gn_col[:, t : t + 1], None, ALU.mult)
 
         nc.scalar.copy(ds[0][:], y_ps[0][:])
         nc.vector.tensor_copy(ds[1][:], y_ps[1][:])
         nc.vector.tensor_copy(ds[2][:], y_ps[2][:])
+        w2 = deal_words("w2", w2_raw, nc.vector.tensor_copy, I32)
         fetch_pair(0)
         fetch_pair(1)
         nc.scalar.copy(ds[3][:], y_ps[3][:])
@@ -173,99 +186,98 @@ def tile_picked_hmixfoldedf_none_po_kernel(
         fetch_pair(3)
         scatter_product(0)
         scatter_product(1)
-        nc.vector.tensor_tensor(ra[:], pa[2][:], sg[2][:], ALU.mult)
-        nc.scalar.activation(ds[2][:].indirect(n2_t[:]), ra[:], ACT.Copy)
-        scale_rows_vector(0)
-        scale_rows_vector(1)
+        nc.vector.tensor_tensor(ra[:], pa[2][:], gate[2][:], ALU.mult)
+        nc.scalar.activation(ds[2][:].indirect(n2_list[:]), ra[:], ACT.Copy)
+        gain_and_round(0)
+        gain_and_round(1)
         scatter_product(3)
-        nc.scalar.activation(z_rows[:, 2, :], ds[2][:], ACT.Copy, scale=gn_t[:, 2:3])
-        scale_rows_vector(3)
-        w23_plane = deal_scales("w23_plane", wraw, nc.gpsimd)
+        nc.scalar.activation(z_rows[:, 2, :], ds[2][:], ACT.Copy, scale=gn_col[:, 2:3])
+        gain_and_round(3)
+
+        w23_plane = deal_scales("w23_plane", nc.gpsimd)
         for t in range(PACK):
             cols = slice(t * P, (t + 1) * P)
             nc.tensor.matmul_mx(
-                out=h_ps[t][:], lhsT=w3[:, cols].bitcast(FP8X4), lhsT_scale=w23_plane[4:P, cols],
+                out=h_ps[t][:], lhsT=w3[:, cols].bitcast(FP8X4), lhsT_scale=w23_plane[W3_PLANE:P, cols],
                 rhs=x2[:].bitcast(FP8X4), rhs_scale=x2_plane[:], start=True, stop=False,
             )
-        z_in = sb("z_in", [P, S, PACK], BF16)
 
-        def weave(copy, dst, src, lo, hi):
+        def weave(name, copy, rows, lo, hi):
+            woven = sb(name, [P, hi - lo, PACK], BF16)
             copy(
-                dst[:, lo:hi, :].rearrange("p (c i) t -> p c t i", i=4),
-                src[:, :, lo:hi].rearrange("p t (c i) -> p c t i", i=4),
+                woven[:].rearrange("p (c i) t -> p c t i", i=RUN),
+                rows[:, :, lo:hi].rearrange("p t (c i) -> p c t i", i=RUN),
             )
+            return woven
 
-        def quantise(codes, plane, src, lo, hi):
+        def quantise(codes, plane, woven, lo, hi):
             nc.vector.quantize_mx(
                 out=codes[:, lo:hi].bitcast(FP8X4), scales=plane[:, lo:hi],
-                in_=src[:, lo:hi, :].rearrange("p j t -> p (j t)"),
+                in_=woven[:].rearrange("p j t -> p (j t)"),
             )
 
-        weave(nc.vector.tensor_copy, z_in, z_rows, 0, HALF)
-        weave(nc.scalar.copy, z_in, z_rows, HALF, S)
-        quantise(z_codes, z_plane, z_in, 0, HALF)
-        quantise(z_codes, z_plane, z_in, HALF, S)
+        z_first = weave("z_first", nc.vector.tensor_copy, z_rows, 0, HALF)
+        z_second = weave("z_second", nc.scalar.copy, z_rows, HALF, COLS)
+        quantise(z_codes, z_plane, z_first, 0, HALF)
+        quantise(z_codes, z_plane, z_second, HALF, COLS)
         for t in range(PACK):
             cols = slice(t * P, (t + 1) * P)
-            for half in range(2):
-                js = slice(half * HALF, (half + 1) * HALF)
+            spans = ((0, HALF), (HALF, COLS)) if t == 0 else ((0, COLS),)
+            for lo, hi in spans:
                 nc.tensor.matmul_mx(
-                    out=h_ps[t][:, js], lhsT=w2[:, cols].bitcast(FP8X4), lhsT_scale=w23_plane[8:P, cols],
-                    rhs=z_codes[:, js].bitcast(FP8X4), rhs_scale=z_plane[:, js], start=False, stop=(half == 1),
+                    out=h_ps[t][:, lo:hi], lhsT=w2[:, cols].bitcast(FP8X4), lhsT_scale=w23_plane[W2_PLANE:P, cols],
+                    rhs=z_codes[:, lo:hi].bitcast(FP8X4), rhs_scale=z_plane[:, lo:hi], start=False, stop=(hi == COLS),
                 )
 
-        ea = [sb("ea%d" % t, [P, S], F32) for t in range(PACK)]
-        ea2 = [sb("ea2%d" % t, [P, S], F32) for t in range(PACK)]
+        ea = [sb("ea%d" % t, [P, COLS], F32) for t in range(PACK)]
+        ea2 = [sb("ea2%d" % t, [P, COLS], F32) for t in range(PACK)]
         top = [sb("top%d" % t, [P, 1], F32) for t in range(PACK)]
         low = [sb("low%d" % t, [P, 1], F32) for t in range(PACK)]
         top_bias = [sb("top_bias%d" % t, [P, 1], F32) for t in range(PACK)]
         low_bias = [sb("low_bias%d" % t, [P, 1], F32) for t in range(PACK)]
-        res = sb("res", [P, PACK, S], F32)
-        o_in = sb("o_in", [P, S, PACK], BF16)
-        o_codes = sb("o_codes", [P, S], U32)
-        o_plane = sb("o_plane", [P, S], U8)
+        result = sb("result", [P, PACK, COLS], F32)
+        out_codes = sb("out_codes", [P, COLS], U32)
+        out_plane = sb("out_plane", [P, COLS], U8)
         out_rows = out_0.rearrange("(p t) j -> p t j", t=PACK)
 
         for t in range(PACK):
-            nc.vector.tensor_scalar(h[t][:, :S], h_ps[t][:], 1.0, None, ALU.mult, ALU.max, accum_out=top[t][:])
+            nc.vector.tensor_scalar(h[t][:, :COLS], h_ps[t][:], 1.0, None, ALU.mult, ALU.max, accum_out=top[t][:])
             nc.gpsimd.tensor_scalar(top_bias[t][:], top[t][:], neg_tau[:, t : t + 1], 0.0, ALU.mult, ALU.add)
             nc.vector.tensor_reduce(low[t][:], h_ps[t][:], AXIS.X, ALU.min)
-            nc.gpsimd.tensor_scalar(low_bias[t][:], low[t][:], tau2_t[:, t : t + 1], 0.0, ALU.mult, ALU.add)
-        both = [sb("both%d" % t, [P, S], F32, "low3" if t == 0 else "") for t in range(PACK)]
+            nc.gpsimd.tensor_scalar(low_bias[t][:], low[t][:], tau2_col[:, t : t + 1], 0.0, ALU.mult, ALU.add)
+        last_low = "low%d" % (PACK - 1)
+        both = [sb("both%d" % t, [P, COLS], F32, last_low if t == 0 else "") for t in range(PACK)]
 
-        def fetch_top(t, lo, hi):
+        def fetch_exponentials(t, lo, hi):
+            entries = slice(lo // LIST_ROWS, hi // LIST_ROWS)
             nc.scalar.activation(
-                ea[t][:, lo:hi], h[t][:].indirect(n3_t[:, lo // 16 : hi // 16]), ACT.Exp,
-                bias=top_bias[t][:], scale=tau_t[:, t : t + 1],
+                ea[t][:, lo:hi], h[t][:].indirect(n3_list[:, entries]), ACT.Exp,
+                bias=top_bias[t][:], scale=tau_col[:, t : t + 1],
             )
-
-        def fetch_low(t, lo, hi):
             nc.scalar.activation(
-                ea2[t][:, lo:hi], h[t][:].indirect(n4_t[:, lo // 16 : hi // 16]), ACT.Exp,
+                ea2[t][:, lo:hi], h[t][:].indirect(n4_list[:, entries]), ACT.Exp,
                 bias=low_bias[t][:], scale=neg_tau2[:, t : t + 1],
             )
 
         def combine(t, lo, hi):
             nc.vector.tensor_tensor(both[t][:, lo:hi], ea[t][:, lo:hi], ea2[t][:, lo:hi], ALU.add)
             nc.vector.scalar_tensor_tensor(
-                res[:, t, lo:hi], h[t][:, lo:hi], 1.5, both[t][:, lo:hi], ALU.mult, ALU.mult
+                result[:, t, lo:hi], h[t][:, lo:hi], 1.5, both[t][:, lo:hi], ALU.mult, ALU.mult
             )
 
-        for t in range(2):
-            fetch_top(t, 0, S)
-            fetch_low(t, 0, S)
-            combine(t, 0, S)
-            nc.sync.dma_start(out_rows[:, t, :], res[:, t, :])
-        codes_out = words_view(out_1)
-        for lo, hi in ((0, 256), (256, 384), (384, 512)):
-            for t in range(2, PACK):
-                fetch_top(t, lo, hi)
-                fetch_low(t, lo, hi)
+        for t in range(WHOLE_TILES):
+            fetch_exponentials(t, 0, COLS)
+            combine(t, 0, COLS)
+            nc.sync.dma_start(out_rows[:, t, :], result[:, t, :])
+        codes_dram = words_view(out_1)
+        for lo, hi in PIECES:
+            for t in range(WHOLE_TILES, PACK):
+                fetch_exponentials(t, lo, hi)
                 combine(t, lo, hi)
-            nc.sync.dma_start(out_rows[:, 2:PACK, lo:hi], res[:, 2:PACK, lo:hi])
-            weave(nc.vector.tensor_copy, o_in, res, lo, hi)
-            quantise(o_codes, o_plane, o_in, lo, hi)
-            nc.sync.dma_start(codes_out[:, lo:hi], o_codes[:, lo:hi].bitcast(I32))
-        for r in range(4):
+            nc.sync.dma_start(out_rows[:, WHOLE_TILES:PACK, lo:hi], result[:, WHOLE_TILES:PACK, lo:hi])
+            out_woven = weave("out_woven%d" % lo, nc.vector.tensor_copy, result, lo, hi)
+            quantise(out_codes, out_plane, out_woven, lo, hi)
+            nc.sync.dma_start(codes_dram[:, lo:hi], out_codes[:, lo:hi].bitcast(I32))
+        for r in range(QUAD_BLOCKS):
             queue = nc.scalar if r % 2 else nc.sync
-            queue.dma_start(out_2[0][r:16:4, :].bitcast(I32), o_plane[r:P:32, :].bitcast(I32))
+            queue.dma_start(out_2[0][r:BLOCKS:QUAD_BLOCKS, :].bitcast(I32), out_plane[r:P:32, :].bitcast(I32))

from contextlib import ExitStack

import concourse.mybir as mybir

F32 = mybir.dt.float32
BF16 = mybir.dt.bfloat16
I32 = mybir.dt.int32
U32 = mybir.dt.uint32
U16 = mybir.dt.uint16
U8 = mybir.dt.uint8
FP8X4 = mybir.dt.float8_e4m3fn_x4
ALU = mybir.AluOpType
ACT = mybir.ActivationFunctionType
AXIS = mybir.AxisListType

P = 128
TOKENS = 2048
COLS = 512
PAIRS = 256
PACK = 4
INT_BYTES = 4
QUADS = 4
QUAD_BLOCKS = 4
BLOCKS = 16
LIST_ROWS = 16
RUN = 4
HALF = COLS // 2
W3_PLANE = 4
W2_PLANE = 8
WHOLE_TILES = 2
PIECES = ((0, 256), (256, 384), (384, 512))
FLOPS = 3 * 2 * 512 * 512 * 512


def words_view(dram):
    return dram[0].rearrange("p n t -> p (n t)").bitcast(I32)


def tile_picked_hmixfoldedf_none_po_kernel(
    tc, x_words, x_scales, w1_words, w1_scales, gn, w2_words, w2_scales, w3_words, w3_scales,
    tau, tau2, offs, n1, n2, two, n3, n4, out_0, out_1, out_2,
):
    nc = tc.nc
    with ExitStack() as ctx:
        keep = ctx.enter_context(tc.tile_pool(name="keep", bufs=1))
        psum = ctx.enter_context(tc.psum_pool(name="psum", bufs=1))

        def sb(name, shape, dtype, tag=""):
            return keep.tile(shape, dtype, name=name, tag=tag or name, align_bytes=64)

        def load_list(name, dram):
            tile = keep.tile(list(dram.shape), U16, name=name)
            nc.sync.dma_start(tile[:], dram)
            return tile

        def load_words(name, dram):
            tile = sb(name, [P, dram.shape[2]], U32)
            nc.sync.dma_start(tile[:].bitcast(I32), words_view(dram))
            return tile

        def load_column(name, dram):
            tile = sb(name, [P, PACK], F32)
            nc.gpsimd.dma_start(tile[:], dram.rearrange("(p t) o -> p (t o)", t=PACK))
            return tile

        warm_in = sb("warm_in", [P, 1], F32)
        warm_out = sb("warm_out", [P, 1], F32)
        nc.vector.memset(warm_in[:], 0.0)
        nc.scalar.activation(warm_out[:], warm_in[:], ACT.Sigmoid)

        offs_list = load_list("offs_list", offs)
        x_scale_rows = sb("x_scale_rows", [P, TOKENS], U8)
        nc.sync.dma_start(
            x_scale_rows[:].bitcast(I32),
            x_scales[0].bitcast(I32).unsqueeze(1).to_broadcast([BLOCKS, P // BLOCKS, TOKENS // INT_BYTES]),
        )
        two_list = load_list("two_list", two)
        w_scale_rows = sb("w_scale_rows", [P, COLS], U8)
        for q in range(QUADS):
            nc.sync.dma_start(
                w_scale_rows[32 * q : 32 * q + 32, :].bitcast(I32),
                w1_scales[0][4 * q : 4 * q + 4, :].bitcast(I32).unsqueeze(0).to_broadcast([8, QUAD_BLOCKS, COLS // INT_BYTES]),
            )
        x_table = load_words("x_table", x_words)
        w1_raw = load_words("w1_raw", w1_words)

        xq_plane = sb("xq_plane", [P, COLS], U8)
        x2_plane = sb("x2_plane", [P, COLS], U8)
        nc.gpsimd.memset(xq_plane[:].bitcast(I32), 0)
        nc.gpsimd.memset(x2_plane[:].bitcast(I32), 0)
        h = [sb("h%d" % t, [P, 2 * COLS if t < WHOLE_TILES else COLS], F32) for t in range(PACK)]
        for t in range(WHOLE_TILES):
            nc.gpsimd.memset(h[t][:, COLS:], 0.0)
        gn_col = load_column("gn_col", gn)
        tau_col = load_column("tau_col", tau)
        tau2_col = load_column("tau2_col", tau2)
        neg_tau = sb("neg_tau", [P, PACK], F32)
        nc.gpsimd.tensor_scalar(neg_tau[:], tau_col[:], -1.0, 0.0, ALU.mult, ALU.add)
        neg_tau2 = sb("neg_tau2", [P, PACK], F32)
        nc.gpsimd.tensor_scalar(neg_tau2[:], tau2_col[:], -1.0, 0.0, ALU.mult, ALU.add)

        def gather_scales(name, offsets, plane, queue):
            picked = sb(name, [P, COLS], U8)
            nc.vector.tensor_copy(picked[:], x_scale_rows[:].indirect(offsets[:]))
            for r in range(QUAD_BLOCKS):
                queue.dma_start(plane[r:P:32, :].bitcast(I32), picked[8 * r : P : 32, :].bitcast(I32))

        def deal_scales(name, engine):
            plane = sb(name, [P, COLS], U8)
            engine.tensor_copy(
                plane[:].rearrange("p (t m) -> p t m", t=PACK),
                w_scale_rows[:].rearrange("p (m t) -> p t m", t=PACK),
            )
            return plane

        def deal_words(name, raw, copy, dtype):
            dealt = sb(name, [P, COLS], U32)
            copy(
                dealt[:].bitcast(dtype).rearrange("p (t c i) -> p c t i", t=PACK, i=RUN),
                raw[:].bitcast(dtype).rearrange("p (c i t) -> p c t i", t=PACK, i=RUN),
            )
            return dealt

        gather_scales("xq_picked", offs_list, xq_plane, nc.scalar)
        w1_plane = deal_scales("w1_plane", nc.vector)
        xq = sb("xq", [P, COLS], U32)
        nc.vector.tensor_copy(xq[:], x_table[:].indirect(offs_list[:]))

        n2_list = load_list("n2_list", n2)
        n1_list = load_list("n1_list", n1)
        w3_raw = load_words("w3_raw", w3_words)
        w2_raw = load_words("w2_raw", w2_words)

        w1 = sb("w1", [P, COLS], U32)
        for t in range(PACK):
            nc.scalar.copy(w1[:, t * P : (t + 1) * P], w1_raw[:, t:COLS:PACK])

        y_ps = [psum.tile([P, COLS], F32, name="y_ps%d" % t) for t in range(PACK)]
        h_ps = [psum.tile([P, COLS], F32, name="h_ps%d" % t) for t in range(PACK)]
        for t in range(PACK):
            cols = slice(t * P, (t + 1) * P)
            nc.tensor.matmul_mx(
                out=y_ps[t][:], lhsT=w1[:, cols].bitcast(FP8X4), lhsT_scale=w1_plane[:, cols],
                rhs=xq[:].bitcast(FP8X4), rhs_scale=xq_plane[:], start=True, stop=True,
            )

        gather_scales("x2_picked", two_list, x2_plane, nc.sync)
        x2 = sb("x2", [P, COLS], U32)
        nc.vector.tensor_copy(x2[:], x_table[:].indirect(two_list[:]))
        w3 = deal_words("w3", w3_raw, nc.scalar.copy, U32)
        for k, dram in ((W3_PLANE, w3_scales), (W2_PLANE, w2_scales)):
            for q in range(QUADS):
                nc.sync.dma_start(
                    w_scale_rows[32 * q + k : 32 * q + k + 4, :].bitcast(I32),
                    dram[0][4 * q : 4 * q + 4, :].bitcast(I32),
                )
        n3_list = load_list("n3_list", n3)
        n4_list = load_list("n4_list", n4)

        ds = [sb("ds%d" % t, [P, COLS], F32) for t in range(PACK)]
        pa = [sb("pa%d" % t, [P, PAIRS], F32) for t in range(PACK)]
        gate = [sb("gate%d" % t, [P, PAIRS], F32) for t in range(PACK)]
        ra = sb("ra", [P, PAIRS], F32)
        z_rows = sb("z_rows", [P, PACK, COLS], BF16)
        z_codes = sb("z_codes", [P, COLS], U32)
        z_plane = sb("z_plane", [P, COLS], U8)

        def fetch_pair(t):
            nc.scalar.activation(gate[t][:], ds[t][:].indirect(n2_list[:]), ACT.Sigmoid)
            nc.scalar.activation(pa[t][:], ds[t][:].indirect(n1_list[:]), ACT.Copy)

        def scatter_product(t):
            nc.vector.tensor_tensor(ds[t][:].indirect(n2_list[:]), pa[t][:], gate[t][:], ALU.mult)

        def gain_and_round(t):
            nc.vector.tensor_scalar(z_rows[:, t, :], ds[t][:], gn_col[:, t : t + 1], None, ALU.mult)

        nc.scalar.copy(ds[0][:], y_ps[0][:])
        nc.vector.tensor_copy(ds[1][:], y_ps[1][:])
        nc.vector.tensor_copy(ds[2][:], y_ps[2][:])
        w2 = deal_words("w2", w2_raw, nc.vector.tensor_copy, I32)
        fetch_pair(0)
        fetch_pair(1)
        nc.scalar.copy(ds[3][:], y_ps[3][:])
        fetch_pair(2)
        fetch_pair(3)
        scatter_product(0)
        scatter_product(1)
        nc.vector.tensor_tensor(ra[:], pa[2][:], gate[2][:], ALU.mult)
        nc.scalar.activation(ds[2][:].indirect(n2_list[:]), ra[:], ACT.Copy)
        gain_and_round(0)
        gain_and_round(1)
        scatter_product(3)
        nc.scalar.activation(z_rows[:, 2, :], ds[2][:], ACT.Copy, scale=gn_col[:, 2:3])
        gain_and_round(3)

        w23_plane = deal_scales("w23_plane", nc.gpsimd)
        for t in range(PACK):
            cols = slice(t * P, (t + 1) * P)
            nc.tensor.matmul_mx(
                out=h_ps[t][:], lhsT=w3[:, cols].bitcast(FP8X4), lhsT_scale=w23_plane[W3_PLANE:P, cols],
                rhs=x2[:].bitcast(FP8X4), rhs_scale=x2_plane[:], start=True, stop=False,
            )

        def weave(name, copy, rows, lo, hi):
            woven = sb(name, [P, hi - lo, PACK], BF16)
            copy(
                woven[:].rearrange("p (c i) t -> p c t i", i=RUN),
                rows[:, :, lo:hi].rearrange("p t (c i) -> p c t i", i=RUN),
            )
            return woven

        def quantise(codes, plane, woven, lo, hi):
            nc.vector.quantize_mx(
                out=codes[:, lo:hi].bitcast(FP8X4), scales=plane[:, lo:hi],
                in_=woven[:].rearrange("p j t -> p (j t)"),
            )

        z_first = weave("z_first", nc.vector.tensor_copy, z_rows, 0, HALF)
        z_second = weave("z_second", nc.scalar.copy, z_rows, HALF, COLS)
        quantise(z_codes, z_plane, z_first, 0, HALF)
        quantise(z_codes, z_plane, z_second, HALF, COLS)
        for t in range(PACK):
            cols = slice(t * P, (t + 1) * P)
            spans = ((0, HALF), (HALF, COLS)) if t == 0 else ((0, COLS),)
            for lo, hi in spans:
                nc.tensor.matmul_mx(
                    out=h_ps[t][:, lo:hi], lhsT=w2[:, cols].bitcast(FP8X4), lhsT_scale=w23_plane[W2_PLANE:P, cols],
                    rhs=z_codes[:, lo:hi].bitcast(FP8X4), rhs_scale=z_plane[:, lo:hi], start=False, stop=(hi == COLS),
                )

        ea = [sb("ea%d" % t, [P, COLS], F32) for t in range(PACK)]
        ea2 = [sb("ea2%d" % t, [P, COLS], F32) for t in range(PACK)]
        top = [sb("top%d" % t, [P, 1], F32) for t in range(PACK)]
        low = [sb("low%d" % t, [P, 1], F32) for t in range(PACK)]
        top_bias = [sb("top_bias%d" % t, [P, 1], F32) for t in range(PACK)]
        low_bias = [sb("low_bias%d" % t, [P, 1], F32) for t in range(PACK)]
        result = sb("result", [P, PACK, COLS], F32)
        out_codes = sb("out_codes", [P, COLS], U32)
        out_plane = sb("out_plane", [P, COLS], U8)
        out_rows = out_0.rearrange("(p t) j -> p t j", t=PACK)

        for t in range(PACK):
            nc.vector.tensor_scalar(h[t][:, :COLS], h_ps[t][:], 1.0, None, ALU.mult, ALU.max, accum_out=top[t][:])
            nc.gpsimd.tensor_scalar(top_bias[t][:], top[t][:], neg_tau[:, t : t + 1], 0.0, ALU.mult, ALU.add)
            nc.vector.tensor_reduce(low[t][:], h_ps[t][:], AXIS.X, ALU.min)
            nc.gpsimd.tensor_scalar(low_bias[t][:], low[t][:], tau2_col[:, t : t + 1], 0.0, ALU.mult, ALU.add)
        last_low = "low%d" % (PACK - 1)
        both = [sb("both%d" % t, [P, COLS], F32, last_low if t == 0 else "") for t in range(PACK)]

        def fetch_exponentials(t, lo, hi):
            entries = slice(lo // LIST_ROWS, hi // LIST_ROWS)
            nc.scalar.activation(
                ea[t][:, lo:hi], h[t][:].indirect(n3_list[:, entries]), ACT.Exp,
                bias=top_bias[t][:], scale=tau_col[:, t : t + 1],
            )
            nc.scalar.activation(
                ea2[t][:, lo:hi], h[t][:].indirect(n4_list[:, entries]), ACT.Exp,
                bias=low_bias[t][:], scale=neg_tau2[:, t : t + 1],
            )

        def combine(t, lo, hi):
            nc.vector.tensor_tensor(both[t][:, lo:hi], ea[t][:, lo:hi], ea2[t][:, lo:hi], ALU.add)
            nc.vector.scalar_tensor_tensor(
                result[:, t, lo:hi], h[t][:, lo:hi], 1.5, both[t][:, lo:hi], ALU.mult, ALU.mult
            )

        for t in range(WHOLE_TILES):
            fetch_exponentials(t, 0, COLS)
            combine(t, 0, COLS)
            nc.sync.dma_start(out_rows[:, t, :], result[:, t, :])
        codes_dram = words_view(out_1)
        for lo, hi in PIECES:
            for t in range(WHOLE_TILES, PACK):
                fetch_exponentials(t, lo, hi)
                combine(t, lo, hi)
            nc.sync.dma_start(out_rows[:, WHOLE_TILES:PACK, lo:hi], result[:, WHOLE_TILES:PACK, lo:hi])
            out_woven = weave("out_woven%d" % lo, nc.vector.tensor_copy, result, lo, hi)
            quantise(out_codes, out_plane, out_woven, lo, hi)
            nc.sync.dma_start(codes_dram[:, lo:hi], out_codes[:, lo:hi].bitcast(I32))
        for r in range(QUAD_BLOCKS):
            queue = nc.scalar if r % 2 else nc.sync
            queue.dma_start(out_2[0][r:BLOCKS:QUAD_BLOCKS, :].bitcast(I32), out_plane[r:P:32, :].bitcast(I32))
